import numpy as np
import ml_dtypes


def mxq(x, axis, fmt="e4m3"):
    dtype, down = {"e4m3": (ml_dtypes.float8_e4m3fn, 7), "e5m2": (ml_dtypes.float8_e5m2, 14)}[fmt]
    v = np.moveaxis(np.asarray(x, np.float32).astype(ml_dtypes.bfloat16).astype(np.float64), axis, -1)
    blocks = v.reshape(v.shape[:-1] + (-1, 32))
    amax = np.abs(blocks).max(-1, keepdims=True)
    byte = np.maximum(np.where(amax > 0, np.frexp(amax)[1] - 1 + 127, 0) - down, 1)
    scale = np.exp2(byte - 127.0)
    codes = (blocks / scale).astype(np.float32).astype(dtype).astype(np.float64)
    return np.moveaxis((codes * scale).reshape(v.shape), -1, axis)


WIDE = False


def mx_kscale(k):
    if not WIDE:
        return np.ones(k)
    levels = np.array([10, -10, 5, -5, 0])
    if k % 512:
        return np.exp2(np.random.permutation(np.resize(levels, k // 32))).repeat(32)
    a = np.empty((k // 512, 16))
    for p in range(k // 512):
        a[p, :8] = np.random.permutation(np.resize(levels, 8))
        for g in range(8):
            far = levels[np.abs(levels - a[p, g]) >= 10]
            a[p, g + 8] = far[np.random.randint(len(far))]
    return np.exp2(a.ravel()).repeat(32)


def f64(x):
    return np.asarray(x).astype(np.float64)


def striped(idx):
    return np.tile(idx.reshape(-1, 16).T, (8, 1)).astype(np.uint16)


def unstriped(offs):
    return offs[:16].T.reshape(-1).astype(np.int64)


def striped8(idx):
    return np.concatenate([x.reshape(-1, 16).T for x in idx]).astype(np.uint16)


def runs(offs, k):
    lists = np.stack([offs[16 * r : 16 * r + 16].T.reshape(-1) for r in range(8)]).astype(np.int64)
    return lists[np.arange(k) % 512 // 64]


def pack_weight(w):
    k, n = w.shape
    w = f64(np.asarray(w, np.float32).astype(ml_dtypes.bfloat16)).reshape(k // 32, 32, n)
    amax = np.abs(w).max(1)
    byte = np.clip(np.where(amax > 0, np.frexp(amax)[1] - 1 + 127 - 7, 1), 1, 254)
    scaled = (w * np.exp2(127.0 - byte)[:, None, :]).reshape(k, n).astype(np.float32)
    words = np.ascontiguousarray(scaled.reshape(k // 512, 128, 4, n).transpose(0, 1, 3, 2)).astype(ml_dtypes.float8_e4m3fn).view(np.uint8)
    return words, np.ascontiguousarray(byte.astype(np.uint8).reshape(k // 512, 16, n))


def unpack_weight(words, scales):
    g, p, n, _ = words.shape
    vals = np.ascontiguousarray(words).view(ml_dtypes.float8_e4m3fn).astype(np.float64) * np.repeat(np.exp2(scales.astype(np.float64) - 127.0), 8, axis=1)[..., None]
    return vals.transpose(0, 1, 3, 2).reshape(g * 512, n)


E2M1 = np.array([0.0, 0.5, 1.0, 1.5, 2.0, 3.0, 4.0, 6.0, -0.0, -0.5, -1.0, -1.5, -2.0, -3.0, -4.0, -6.0])


def pack_fp4(w):
    k, n = w.shape
    w = f64(np.asarray(w, np.float32).astype(ml_dtypes.bfloat16)).reshape(k // 32, 32, n)
    amax = np.abs(w).max(1)
    mant, ex = np.frexp(amax / 6.0)
    byte = np.clip(np.where(amax > 0, np.where(mant > 0.5, ex, ex - 1) + 127, 1), 1, 254)
    scaled = (w * np.exp2(127.0 - byte)[:, None, :]).reshape(k, n).astype(np.float32)
    c = np.ascontiguousarray(scaled.reshape(k // 512, 128, 4, n).transpose(0, 1, 3, 2)).astype(ml_dtypes.float4_e2m1fn).view(np.uint8) & 0xF
    words = (c[..., 0::2] | (c[..., 1::2] << 4)).reshape(k // 512, 128, 2 * n)
    return np.ascontiguousarray(words), np.ascontiguousarray(byte.astype(np.uint8).reshape(k // 512, 16, n))


def unpack_fp4(words, scales):
    g, _, n = scales.shape
    words = np.ascontiguousarray(words).reshape(g, 128, n, 2)
    nib = np.empty((g, 128, n, 4), np.uint8)
    nib[..., 0::2] = words & 0xF
    nib[..., 1::2] = words >> 4
    vals = E2M1[nib] * np.repeat(np.exp2(scales.astype(np.float64) - 127.0), 8, axis=1)[..., None]
    return vals.transpose(0, 1, 3, 2).reshape(g * 512, n)


def planes(y):
    n, m = y.shape
    v = y.astype(np.float32).astype(ml_dtypes.bfloat16).astype(np.float64).reshape(n // 32, 32, m)
    top = np.abs(v).max(1)
    byte = np.clip(np.where(top > 0, np.frexp(top)[1] - 1 + 127 - 7, 1), 1, 254)
    codes = (v * np.exp2(127.0 - byte)[:, None, :]).reshape(n, m).astype(np.float32).astype(ml_dtypes.float8_e4m3fn).view(np.uint8)
    words = codes.reshape(n // 512, 128, 4, m).transpose(0, 1, 3, 2)
    return np.ascontiguousarray(words), np.ascontiguousarray(byte.astype(np.uint8).reshape(n // 512, 16, m))


K, T, S, N, H, W = 512, 2048, 512, 512, 512, 256


def setup_inputs():
    n = np.random.standard_normal
    s = mx_kscale(K)[:, None]
    u = mx_kscale(H)
    packed_xT = pack_weight(n((K, T)) * s)
    packed_w1 = pack_fp4(n((K, H)) / np.sqrt(K) / s)
    packed_w2 = pack_fp4(n((H, N)) / np.sqrt(2 * H) / u[:, None])
    packed_w3 = pack_fp4(n((H, N)) / np.sqrt(2 * H) / u[:, None])
    perm = np.stack([np.random.permutation(S) for _ in range(8)])
    return {
        "x_words": packed_xT[0],
        "x_scales": packed_xT[1],
        "w1_words": packed_w1[0],
        "w1_scales": packed_w1[1],
        "gn": (np.random.uniform(0.5, 1.5, (H, 1)) * u[:, None]).astype(np.float32),
        "gm": (np.random.uniform(0.5, 1.5, (H, 1)) * u[:, None]).astype(np.float32),
        "w2_words": packed_w2[0],
        "w2_scales": packed_w2[1],
        "w3_words": packed_w3[0],
        "w3_scales": packed_w3[1],
        "offs": striped(np.random.permutation(T)[:S]),
        "n1": striped8(np.stack([np.random.permutation(S) for _ in range(8)])),
        "n2": striped8(perm[:, :W]),
        "n3": striped8(perm[:, W:]),
        "n4": striped8(np.stack([np.random.permutation(S) for _ in range(8)])),
        "n5": striped8(np.stack([np.random.permutation(S) for _ in range(8)])),
    }


def reference(x_words, x_scales, w1_words, w1_scales, gn, gm, w2_words, w2_scales, w3_words, w3_scales, offs, n1, n2, n3, n4, n5):
    xq = unpack_weight(x_words, x_scales)[:, unstriped(offs)]
    y = unpack_fp4(w1_words, w1_scales).T @ xq
    z = f64(gn) * (np.maximum(y, y[np.arange(H)[:, None], runs(n1, H)]))
    pb = y[np.arange(H)[:, None], runs(n3, H)]
    pa = y[np.arange(H)[:, None], runs(n2, H)]
    rb = pb - (0.5 * pa)
    ra = np.sqrt((pa) ** 2 + (pb) ** 2 + 0.25)
    ds = np.zeros((H, S))
    ds[np.arange(H)[:, None], runs(n2, H)] = ra
    dt = ds.copy()
    dt[np.arange(H)[:, None], runs(n3, H)] = rb
    z2 = f64(gm) * dt
    h = unpack_fp4(w2_words, w2_scales).T @ mxq(z, 0, "e4m3") + unpack_fp4(w3_words, w3_scales).T @ mxq(z2, 0, "e4m3")
    out_0 = h - (np.minimum(h[np.arange(N)[:, None], runs(n4, N)], h[np.arange(N)[:, None], runs(n5, N)]))
    return (out_0,) + planes(out_0)

@@ -1,0 +1,249 @@
+from contextlib import ExitStack
+
+import concourse.mybir as mybir
+from concourse.masks import make_identity
+
+K, T, S, N, H, W = 512, 2048, 512, 512, 512, 256
+FLOPS = 2 * K * H * S + 2 * 2 * H * N * S
+
+F32 = mybir.dt.float32
+BF16 = mybir.dt.bfloat16
+I32 = mybir.dt.int32
+U32 = mybir.dt.uint32
+U16 = mybir.dt.uint16
+U8 = mybir.dt.uint8
+FP8X4 = mybir.dt.float8_e4m3fn_x4
+FP4X4 = mybir.dt.float4_e2m1fn_x4
+ALU = mybir.AluOpType
+ACT = mybir.ActivationFunctionType
+
+P = 128
+PACK = 4
+CHUNKS = ((0, 256), (256, 384), (384, 512))
+HALVES = ((0, 256), (256, 512))
+
+
+def tile_picked_joinbigpolarunder_none_po_kernel(
+    tc, x_words, x_scales, w1_words, w1_scales, gn, gm, w2_words, w2_scales, w3_words, w3_scales,
+    offs, n1, n2, n3, n4, n5, out_0, out_1, out_2,
+):
+    nc = tc.nc
+    with ExitStack() as ctx:
+        keep = ctx.enter_context(tc.tile_pool(name="keep", bufs=1))
+        psum = ctx.enter_context(tc.psum_pool(name="psum", bufs=1))
+
+        def load_list(name, src):
+            tile = keep.tile([P, src.shape[1]], U16, name=name)
+            nc.sync.dma_start(tile[:], src)
+            return tile
+
+        def load_scales(queues, name, src):
+            tile = keep.tile([P, src.shape[2]], U8, name=name, tag=name, align_bytes=64)
+            nc.gpsimd.memset(tile[:].bitcast(I32), 0)
+            for q, queue in enumerate(queues):
+                queue.dma_start(tile[32 * q : 32 * q + 4, :].bitcast(I32), src[0, 4 * q : 4 * q + 4, :].bitcast(I32))
+            return tile
+
+        def load_words(name, tag, src):
+            tile = keep.tile([P, src.shape[2]], U8, name=name, tag=tag, align_bytes=64)
+            nc.sync.dma_start(tile[:].bitcast(I32), src[0].bitcast(I32))
+            return tile
+
+        def load_gain(name, src):
+            tile = keep.tile([P, PACK], F32, name=name)
+            nc.gpsimd.dma_start(tile[:], src.rearrange("(p t) o -> p (t o)", t=PACK))
+            return tile
+
+        def deal_words(name, tag, raw, t0, t1):
+            tile = keep.tile([P, (t1 - t0) * 2 * P], U8, name=name, tag=tag, align_bytes=64)
+            nc.vector.tensor_copy(
+                tile[:].rearrange("p (t m b) -> p t m b", m=P, b=2),
+                raw[:].rearrange("p (m t b) -> p t m b", t=PACK, b=2)[:, t0:t1],
+            )
+            return tile
+
+        def deal_scales(name, tag, raw, t0, t1):
+            tile = keep.tile([P, (t1 - t0) * P], U8, name=name, tag=tag, align_bytes=64)
+            nc.vector.tensor_copy(
+                tile[:].rearrange("p (t m) -> p t m", m=P),
+                raw[:].rearrange("p (m t) -> p t m", t=PACK)[:, t0:t1],
+            )
+            return tile
+
+        def mx_pass(bank, words, scales, t, codes, code_scales, start, stop):
+            nc.tensor.matmul_mx(
+                out=bank,
+                lhsT=words[:, 2 * P * t : 2 * P * (t + 1)].bitcast(FP4X4),
+                lhsT_scale=scales[:, P * t : P * (t + 1)],
+                rhs=codes.bitcast(FP8X4),
+                rhs_scale=code_scales,
+                start=start,
+                stop=stop,
+            )
+
+        offs_t = load_list("offs_t", offs)
+        n2_t = load_list("n2_t", n2)
+        n3_t = load_list("n3_t", n3)
+        n1_t = load_list("n1_t", n1)
+        w1_raw = load_words("w1_raw", "w1_raw", w1_words)
+        n4_t = load_list("n4_t", n4)
+        n5_t = load_list("n5_t", n5)
+        x_raw = keep.tile([P, T], I32, name="x_raw", tag="x_raw", align_bytes=64)
+        nc.sync.dma_start(x_raw[:], x_words[0].rearrange("p n r -> p (n r)").bitcast(I32))
+        xs_raw = load_scales([nc.scalar] * 4, "xs_raw", x_scales)
+        w1s_raw = load_scales([nc.scalar] * 3 + [nc.gpsimd], "w1s_raw", w1_scales)
+        ident = keep.tile([P, P], F32, name="ident")
+        make_identity(nc, ident[:])
+        w3s_raw = load_scales([nc.sync] * 4, "w3s_raw", w3_scales)
+        w2s_raw = load_scales([nc.sync] * 4, "w2s_raw", w2_scales)
+        gm_t = load_gain("gm_t", gm)
+        gn_t = load_gain("gn_t", gn)
+
+        w1 = deal_words("w1", "w1", w1_raw, 0, PACK)
+        w3_raw = load_words("w3_raw", "w1_raw", w3_words)
+        xs = keep.tile([P, S], U8, name="xs", align_bytes=64)
+        nc.vector.tensor_copy(xs[:], xs_raw[:].indirect(offs_t[:]))
+        w2_raw = load_words("w2_raw", "xs_raw", w2_words)
+        w1s = deal_scales("w1s", "w1s", w1s_raw, 0, PACK)
+        xw = keep.tile([P, S], U32, name="xw", align_bytes=64)
+        nc.vector.tensor_copy(xw[:], x_raw[:].bitcast(U32).indirect(offs_t[:]))
+
+        y = []
+        for t in range(PACK):
+            bank = psum.tile([P, S], F32, name=f"ybank{t}", tag=f"bank{t}")
+            mx_pass(bank[:], w1, w1s, t, xw[:], xs[:], True, True)
+            y_t = keep.tile([P, S], F32, name=f"y{t}")
+            nc.scalar.copy(y_t[:], bank[:])
+            y.append(y_t)
+
+        w3 = deal_words("w3", "x_raw", w3_raw, 0, PACK)
+        w3s = deal_scales("w3s", "w1_raw", w3s_raw, 0, PACK)
+        w2_first = deal_words("w2_first", "w3s_raw", w2_raw, 0, 1)
+        w2s = deal_scales("w2s", "w2s", w2s_raw, 0, PACK)
+
+        z2_bf = keep.tile([P, S, PACK], BF16, name="z2_bf", align_bytes=64)
+        ra, dt = [], []
+
+        def pair_up(t):
+            u = keep.tile([P, W], F32, name=f"half_pa{t}")
+            nc.vector.tensor_scalar(u[:], y[t][:].indirect(n2_t[:]), -0.5, 0.0, ALU.mult, ALU.add)
+            b = keep.tile([P, W], F32, name=f"pb{t}")
+            nc.vector.tensor_copy(b[:], y[t][:].indirect(n3_t[:]))
+            sq = keep.tile([P, 2, W], F32, name=f"sq{t}")
+            nc.scalar.activation(sq[:, 0, :], u[:], ACT.Square, scale=2.0)
+            nc.scalar.activation(sq[:, 1, :], b[:], ACT.Square)
+            bank = psum.tile([P, 2, W], F32, name=f"rbank{t}", tag=f"bank{t}")
+            for a in range(0, W, P):
+                for e in range(2):
+                    nc.tensor.matmul(bank[:, 0, a : a + P], sq[:, e, a : a + P], ident[:], start=e == 0, stop=e == 1, is_transpose=True)
+            turned = keep.tile([P, W], F32, name=f"turned{t}")
+            nc.scalar.activation(turned[:], bank[:, 0, :], ACT.Sqrt, bias=0.25)
+            for a in range(0, W, P):
+                nc.tensor.transpose(bank[:, 1, a : a + P], turned[:, a : a + P], ident[:])
+            r = keep.tile([P, W], F32, name=f"ra{t}", tag=f"ra{t}")
+            nc.scalar.copy(r[:], bank[:, 1, :])
+            ra.append(r)
+            return u, b
+
+        def put_rb(t, u, b):
+            d = keep.tile([P, S], F32, name=f"dt{t}")
+            nc.vector.tensor_tensor(d[:].indirect(n3_t[:]), b[:], u[:], ALU.add)
+            dt.append(d)
+
+        def put_ra(t):
+            nc.vector.tensor_copy(dt[t][:].indirect(n2_t[:]), ra[t][:])
+            nc.scalar.activation(z2_bf[:, :, t], dt[t][:], ACT.Copy, scale=gm_t[:, t : t + 1])
+
+        for t in range(PACK):
+            u, b = pair_up(t)
+            if t > 0:
+                put_ra(t - 1)
+            put_rb(t, u, b)
+        put_ra(PACK - 1)
+        z2_codes = keep.tile([P, S], U32, name="z2_codes", align_bytes=64)
+        z2_scales = keep.tile([P, S], U8, name="z2_scales", align_bytes=64)
+        nc.vector.quantize_mx(
+            out=z2_codes[:].bitcast(FP8X4), scales=z2_scales[:], in_=z2_bf[:].rearrange("p j t -> p (j t)")
+        )
+
+        z_codes = keep.tile([P, S], U32, name="z_codes", align_bytes=64)
+        z_scales = keep.tile([P, S], U8, name="z_scales", align_bytes=64)
+        z_bf = [keep.tile([P, j1 - j0, PACK], BF16, name=f"z_bf{c}", tag=f"z_bf{c}", align_bytes=64) for c, (j0, j1) in enumerate(CHUNKS)]
+        h = [keep.tile([P, S], F32, name=f"h{t}") for t in range(PACK)]
+        neg_h = [keep.tile([P, S], F32, name=f"neg_h{t}") for t in range(PACK)]
+        for t in range(PACK - 1):
+            g = keep.tile([P, S], F32, name=f"g{t}", tag=("ra2", "ra3", "ra2")[t])
+            for j0, j1 in HALVES:
+                nc.vector.tensor_copy(g[:, j0:j1], y[t][:].indirect(n1_t[:, j0 // 16 : j1 // 16]))
+            m = keep.tile([P, S], F32, name=f"m{t}")
+            nc.vector.tensor_tensor(m[:], g[:], y[t][:], ALU.max)
+            for c, (j0, j1) in enumerate(CHUNKS):
+                nc.scalar.activation(z_bf[c][:, :, t], m[:, j0:j1], ACT.Copy, scale=gn_t[:, t : t + 1])
+        last = PACK - 1
+        g = keep.tile([P, S], F32, name="g3", tag="ra3")
+        m = keep.tile([P, S], F32, name="m3")
+        for c, (j0, j1) in enumerate(CHUNKS):
+            width = j1 - j0
+            nc.vector.tensor_copy(g[:, j0:j1], y[last][:].indirect(n1_t[:, j0 // 16 : j1 // 16]))
+            nc.vector.tensor_tensor(m[:, j0:j1], g[:, j0:j1], y[last][:, j0:j1], ALU.max)
+            nc.scalar.activation(z_bf[c][:, :, last], m[:, j0:j1], ACT.Copy, scale=gn_t[:, last : last + 1])
+            nc.vector.quantize_mx(
+                out=z_codes[:, j0:j1].bitcast(FP8X4), scales=z_scales[:, j0:j1],
+                in_=z_bf[c][:].rearrange("p j t -> p (j t)"),
+            )
+            bank = psum.tile([P, width], F32, name=f"h0bank{c}", tag=f"h0bank{c}")
+            for a in range(j0, j1, P):
+                cols = slice(a, a + P)
+                mx_pass(bank[:, a - j0 : a - j0 + P], w3, w3s, 0, z2_codes[:, cols], z2_scales[:, cols], True, False)
+                mx_pass(bank[:, a - j0 : a - j0 + P], w2_first, w2s, 0, z_codes[:, cols], z_scales[:, cols], False, True)
+            nc.scalar.activation(neg_h[0][:, j0:j1], bank[:], ACT.Copy, scale=-1.0)
+            nc.scalar.copy(h[0][:, j0:j1], bank[:])
+
+        w2_rest = deal_words("w2_rest", f"z_bf{len(CHUNKS) - 1}", w2_raw, 1, PACK)
+        for t in range(1, PACK):
+            bank = psum.tile([P, S], F32, name=f"hbank{t}", tag=f"bank{t}")
+            mx_pass(bank[:], w3, w3s, t, z2_codes[:], z2_scales[:], True, False)
+            mx_pass(bank[:], w2_rest, w2s[:, P:], t - 1, z_codes[:], z_scales[:], False, True)
+            nc.scalar.activation(neg_h[t][:], bank[:], ACT.Copy, scale=-1.0)
+            nc.scalar.copy(h[t][:], bank[:])
+
+        out_rows = out_0.rearrange("(p t) j -> p t j", t=PACK)
+        out_words = out_1[0].rearrange("p j r -> p (j r)").bitcast(I32)
+        o_codes = keep.tile([P, S], I32, name="o_codes", align_bytes=64)
+        o_scales = keep.tile([P, S], U8, name="o_scales", align_bytes=64)
+        o_bf = [keep.tile([P, j1 - j0, PACK], BF16, name=f"o_bf{c}", align_bytes=64) for c, (j0, j1) in enumerate(CHUNKS)]
+        o = [keep.tile([P, 2, S], F32, name=f"o{u}") for u in range(2)]
+
+        def differences(t, a, b, j0, j1):
+            nc.vector.tensor_tensor(a[:, j0:j1], neg_h[t][:].indirect(n4_t[:, j0 // 16 : j1 // 16]), h[t][:, j0:j1], ALU.add)
+            nc.vector.tensor_tensor(b[:, j0:j1], neg_h[t][:].indirect(n5_t[:, j0 // 16 : j1 // 16]), h[t][:, j0:j1], ALU.add)
+
+        def round_pair(u, c):
+            j0, j1 = CHUNKS[c]
+            nc.scalar.copy(o_bf[c][:, :, 2 * u : 2 * u + 2], o[u][:, :, j0:j1].rearrange("p e j -> p j e"))
+
+        for t in range(PACK - 1):
+            a = keep.tile([P, S], F32, name=f"a{t}")
+            b = keep.tile([P, S], F32, name=f"b{t}")
+            for j0, j1 in HALVES:
+                differences(t, a, b, j0, j1)
+            nc.vector.tensor_tensor(o[t // 2][:, t % 2, :], a[:], b[:], ALU.max)
+            nc.sync.dma_start(out_rows[:, t, :], o[t // 2][:, t % 2, :])
+            if t == 1:
+                for c in range(len(CHUNKS)):
+                    round_pair(0, c)
+        a = keep.tile([P, S], F32, name="a3")
+        b = keep.tile([P, S], F32, name="b3")
+        for c, (j0, j1) in enumerate(CHUNKS):
+            differences(last, a, b, j0, j1)
+            nc.vector.tensor_tensor(o[1][:, 1, j0:j1], a[:, j0:j1], b[:, j0:j1], ALU.max)
+            nc.sync.dma_start(out_rows[:, last, j0:j1], o[1][:, 1, j0:j1])
+            round_pair(1, c)
+            nc.vector.quantize_mx(
+                out=o_codes[:, j0:j1].bitcast(FP8X4), scales=o_scales[:, j0:j1],
+                in_=o_bf[c][:].rearrange("p j t -> p (j t)"),
+            )
+            nc.sync.dma_start(out_words[:, j0:j1], o_codes[:, j0:j1])
+        for q in range(4):
+            queue = nc.scalar if q % 2 else nc.sync
+            queue.dma_start(out_2[0, 4 * q : 4 * q + 4, :].bitcast(I32), o_scales[32 * q : 32 * q + 4, :].bitcast(I32))

@@ -37,12 +37,14 @@ def tile_picked_joinbigpolarunder_none_po_kernel(
             nc.sync.dma_start(tile[:], src)
             return tile
 
-        def load_scales(queues, name, src):
-            tile = keep.tile([P, src.shape[2]], U8, name=name, tag=name, align_bytes=64)
+        def zeroed_plane(name, tag, width):
+            tile = keep.tile([P, width], U8, name=name, tag=tag, align_bytes=64)
             nc.gpsimd.memset(tile[:].bitcast(I32), 0)
+            return tile
+
+        def load_scales(queues, tile, src):
             for q, queue in enumerate(queues):
                 queue.dma_start(tile[32 * q : 32 * q + 4, :].bitcast(I32), src[0, 4 * q : 4 * q + 4, :].bitcast(I32))
-            return tile
 
         def load_words(name, tag, src):
             tile = keep.tile([P, src.shape[2]], U8, name=name, tag=tag, align_bytes=64)
@@ -82,84 +84,88 @@ def tile_picked_joinbigpolarunder_none_po_kernel(
             )
 
         offs_t = load_list("offs_t", offs)
+        w1_raw = load_words("w1_raw", "w1_raw", w1_words)
+        x_raw = keep.tile([P, T], I32, name="x_raw", tag="x_raw", align_bytes=64)
+        nc.sync.dma_start(x_raw[:], x_words[0].rearrange("p n r -> p (n r)").bitcast(I32))
         n2_t = load_list("n2_t", n2)
         n3_t = load_list("n3_t", n3)
         n1_t = load_list("n1_t", n1)
-        w1_raw = load_words("w1_raw", "w1_raw", w1_words)
         n4_t = load_list("n4_t", n4)
         n5_t = load_list("n5_t", n5)
-        x_raw = keep.tile([P, T], I32, name="x_raw", tag="x_raw", align_bytes=64)
-        nc.sync.dma_start(x_raw[:], x_words[0].rearrange("p n r -> p (n r)").bitcast(I32))
-        xs_raw = load_scales([nc.scalar] * 4, "xs_raw", x_scales)
-        w1s_raw = load_scales([nc.scalar] * 3 + [nc.gpsimd], "w1s_raw", w1_scales)
-        ident = keep.tile([P, P], F32, name="ident")
+        xs_raw = zeroed_plane("xs_raw", "xs_raw", T)
+        w1s_raw = zeroed_plane("w1s_raw", "w1s_raw", H)
+        load_scales([nc.scalar, nc.scalar, nc.gpsimd, nc.gpsimd], xs_raw, x_scales)
+        load_scales([nc.scalar] * 4, w1s_raw, w1_scales)
+        ident = keep.tile([P, P], F32, name="ident", tag="ident", align_bytes=64)
         make_identity(nc, ident[:])
-        w3s_raw = load_scales([nc.sync] * 4, "w3s_raw", w3_scales)
-        w2s_raw = load_scales([nc.sync] * 4, "w2s_raw", w2_scales)
         gm_t = load_gain("gm_t", gm)
         gn_t = load_gain("gn_t", gn)
 
         w1 = deal_words("w1", "w1", w1_raw, 0, PACK)
         w3_raw = load_words("w3_raw", "w1_raw", w3_words)
-        xs = keep.tile([P, S], U8, name="xs", align_bytes=64)
-        nc.vector.tensor_copy(xs[:], xs_raw[:].indirect(offs_t[:]))
-        w2_raw = load_words("w2_raw", "xs_raw", w2_words)
-        w1s = deal_scales("w1s", "w1s", w1s_raw, 0, PACK)
         xw = keep.tile([P, S], U32, name="xw", align_bytes=64)
         nc.vector.tensor_copy(xw[:], x_raw[:].bitcast(U32).indirect(offs_t[:]))
+        xs = keep.tile([P, S], U8, name="xs", tag="x_raw", align_bytes=64)
+        nc.vector.tensor_copy(xs[:], xs_raw[:].indirect(offs_t[:]))
+        w1s_first = deal_scales("w1s_first", "w1s_first", w1s_raw, 0, 1)
+        w1s_rest = deal_scales("w1s_rest", "xs_raw", w1s_raw, 1, PACK)
+        w3 = deal_words("w3", "w1s_raw", w3_raw, 0, PACK)
+        w2_raw = load_words("w2_raw", "w1_raw", w2_words)
 
         y = []
         for t in range(PACK):
             bank = psum.tile([P, S], F32, name=f"ybank{t}", tag=f"bank{t}")
-            mx_pass(bank[:], w1, w1s, t, xw[:], xs[:], True, True)
+            scales = w1s_first[:] if t == 0 else w1s_rest[:, P * (t - 1) : P * t]
+            mx_pass(bank[:], w1[:, 2 * P * t :], scales, 0, xw[:], xs[:], True, True)
             y_t = keep.tile([P, S], F32, name=f"y{t}")
             nc.scalar.copy(y_t[:], bank[:])
             y.append(y_t)
 
-        w3 = deal_words("w3", "x_raw", w3_raw, 0, PACK)
-        w3s = deal_scales("w3s", "w1_raw", w3s_raw, 0, PACK)
-        w2_first = deal_words("w2_first", "w3s_raw", w2_raw, 0, 1)
-        w2s = deal_scales("w2s", "w2s", w2s_raw, 0, PACK)
+        w3s_raw = zeroed_plane("w3s_raw", "w1s_first", N)
+        w2s_raw = zeroed_plane("w2s_raw", "w1", N)
+        load_scales([nc.sync] * 4, w3s_raw, w3_scales)
+        load_scales([nc.sync] * 4, w2s_raw, w2_scales)
 
-        z2_bf = keep.tile([P, S, PACK], BF16, name="z2_bf", align_bytes=64)
-        ra, dt = [], []
+        dt = []
 
         def pair_up(t):
             u = keep.tile([P, W], F32, name=f"half_pa{t}")
             nc.vector.tensor_scalar(u[:], y[t][:].indirect(n2_t[:]), -0.5, 0.0, ALU.mult, ALU.add)
             b = keep.tile([P, W], F32, name=f"pb{t}")
             nc.vector.tensor_copy(b[:], y[t][:].indirect(n3_t[:]))
-            sq = keep.tile([P, 2, W], F32, name=f"sq{t}")
-            nc.scalar.activation(sq[:, 0, :], u[:], ACT.Square, scale=2.0)
-            nc.scalar.activation(sq[:, 1, :], b[:], ACT.Square)
+            sq = keep.tile([P, S], F32, name=f"sq{t}", tag=f"sq{t}", align_bytes=64)
+            nc.scalar.activation(sq[:, :W], u[:], ACT.Square, scale=2.0)
+            nc.scalar.activation(sq[:, W:], b[:], ACT.Square)
             bank = psum.tile([P, 2, W], F32, name=f"rbank{t}", tag=f"bank{t}")
             for a in range(0, W, P):
                 for e in range(2):
-                    nc.tensor.matmul(bank[:, 0, a : a + P], sq[:, e, a : a + P], ident[:], start=e == 0, stop=e == 1, is_transpose=True)
-            turned = keep.tile([P, W], F32, name=f"turned{t}")
+                    nc.tensor.matmul(bank[:, 0, a : a + P], sq[:, e * W + a : e * W + a + P], ident[:], start=e == 0, stop=e == 1, is_transpose=True)
+            turned = keep.tile([P, W], F32, name=f"turned{t}", tag=f"turned{t}", align_bytes=64)
             nc.scalar.activation(turned[:], bank[:, 0, :], ACT.Sqrt, bias=0.25)
             for a in range(0, W, P):
                 nc.tensor.transpose(bank[:, 1, a : a + P], turned[:, a : a + P], ident[:])
             r = keep.tile([P, W], F32, name=f"ra{t}", tag=f"ra{t}")
             nc.scalar.copy(r[:], bank[:, 1, :])
-            ra.append(r)
-            return u, b
+            return u, b, r
 
         def put_rb(t, u, b):
-            d = keep.tile([P, S], F32, name=f"dt{t}")
+            d = keep.tile([P, S], F32, name=f"dt{t}", tag=("sq0", "sq1", "turned0", "turned1")[t], align_bytes=64)
             nc.vector.tensor_tensor(d[:].indirect(n3_t[:]), b[:], u[:], ALU.add)
             dt.append(d)
 
-        def put_ra(t):
-            nc.vector.tensor_copy(dt[t][:].indirect(n2_t[:]), ra[t][:])
+        def put_ra(t, r):
+            nc.vector.tensor_copy(dt[t][:].indirect(n2_t[:]), r)
             nc.scalar.activation(z2_bf[:, :, t], dt[t][:], ACT.Copy, scale=gm_t[:, t : t + 1])
 
+        pairs = [pair_up(t) for t in range(PACK)]
         for t in range(PACK):
-            u, b = pair_up(t)
-            if t > 0:
-                put_ra(t - 1)
-            put_rb(t, u, b)
-        put_ra(PACK - 1)
+            put_rb(t, pairs[t][0], pairs[t][1])
+        z2_bf = keep.tile([P, S, PACK], BF16, name="z2_bf", tag="ident", align_bytes=64)
+        for t in range(PACK):
+            put_ra(t, pairs[t][2][:])
+        w2_first = deal_words("w2_first", "sq1", w2_raw, 0, 1)
+        w2s = deal_scales("w2s", "turned0", w2s_raw, 0, PACK)
+        w3s = deal_scales("w3s", "turned1", w3s_raw, 0, PACK)
         z2_codes = keep.tile([P, S], U32, name="z2_codes", align_bytes=64)
         z2_scales = keep.tile([P, S], U8, name="z2_scales", align_bytes=64)
         nc.vector.quantize_mx(
@@ -169,19 +175,21 @@ def tile_picked_joinbigpolarunder_none_po_kernel(
         z_codes = keep.tile([P, S], U32, name="z_codes", align_bytes=64)
         z_scales = keep.tile([P, S], U8, name="z_scales", align_bytes=64)
         z_bf = [keep.tile([P, j1 - j0, PACK], BF16, name=f"z_bf{c}", tag=f"z_bf{c}", align_bytes=64) for c, (j0, j1) in enumerate(CHUNKS)]
-        h = [keep.tile([P, S], F32, name=f"h{t}") for t in range(PACK)]
-        neg_h = [keep.tile([P, S], F32, name=f"neg_h{t}") for t in range(PACK)]
+        last = PACK - 1
+        neg_h = [keep.tile([P, 2 * S if t < last else S], F32, name=f"neg_h{t}") for t in range(PACK)]
+        h = [neg_h[1][:, S:], neg_h[2][:, S:], keep.tile([P, S], F32, name="h2")[:], keep.tile([P, S], F32, name="h3")[:]]
+        fetched = keep.tile([P, PACK, S], F32, name="fetched", tag="ra3")
         for t in range(PACK - 1):
-            g = keep.tile([P, S], F32, name=f"g{t}", tag=("ra2", "ra3", "ra2")[t])
+            g = fetched[:, t, :]
             for j0, j1 in HALVES:
                 nc.vector.tensor_copy(g[:, j0:j1], y[t][:].indirect(n1_t[:, j0 // 16 : j1 // 16]))
-            m = keep.tile([P, S], F32, name=f"m{t}")
-            nc.vector.tensor_tensor(m[:], g[:], y[t][:], ALU.max)
+            m = neg_h[0][:, S:] if t == 0 else keep.tile([P, S], F32, name=f"m{t}")[:]
+            nc.vector.tensor_tensor(m, g, y[t][:], ALU.max)
             for c, (j0, j1) in enumerate(CHUNKS):
                 nc.scalar.activation(z_bf[c][:, :, t], m[:, j0:j1], ACT.Copy, scale=gn_t[:, t : t + 1])
-        last = PACK - 1
-        g = keep.tile([P, S], F32, name="g3", tag="ra3")
+        g = fetched[:, last, :]
         m = keep.tile([P, S], F32, name="m3")
+        banks = []
         for c, (j0, j1) in enumerate(CHUNKS):
             width = j1 - j0
             nc.vector.tensor_copy(g[:, j0:j1], y[last][:].indirect(n1_t[:, j0 // 16 : j1 // 16]))
@@ -196,16 +204,18 @@ def tile_picked_joinbigpolarunder_none_po_kernel(
                 cols = slice(a, a + P)
                 mx_pass(bank[:, a - j0 : a - j0 + P], w3, w3s, 0, z2_codes[:, cols], z2_scales[:, cols], True, False)
                 mx_pass(bank[:, a - j0 : a - j0 + P], w2_first, w2s, 0, z_codes[:, cols], z_scales[:, cols], False, True)
-            nc.scalar.activation(neg_h[0][:, j0:j1], bank[:], ACT.Copy, scale=-1.0)
-            nc.scalar.copy(h[0][:, j0:j1], bank[:])
+            banks.append(bank)
+        for c, (j0, j1) in enumerate(CHUNKS):
+            nc.scalar.activation(neg_h[0][:, j0:j1], banks[c][:], ACT.Copy, scale=-1.0)
+            nc.scalar.copy(h[0][:, j0:j1], banks[c][:])
 
         w2_rest = deal_words("w2_rest", f"z_bf{len(CHUNKS) - 1}", w2_raw, 1, PACK)
         for t in range(1, PACK):
             bank = psum.tile([P, S], F32, name=f"hbank{t}", tag=f"bank{t}")
             mx_pass(bank[:], w3, w3s, t, z2_codes[:], z2_scales[:], True, False)
             mx_pass(bank[:], w2_rest, w2s[:, P:], t - 1, z_codes[:], z_scales[:], False, True)
-            nc.scalar.activation(neg_h[t][:], bank[:], ACT.Copy, scale=-1.0)
-            nc.scalar.copy(h[t][:], bank[:])
+            nc.scalar.activation(neg_h[t][:, :S], bank[:], ACT.Copy, scale=-1.0)
+            nc.scalar.copy(h[t], bank[:])
 
         out_rows = out_0.rearrange("(p t) j -> p t j", t=PACK)
         out_words = out_1[0].rearrange("p j r -> p (j r)").bitcast(I32)
@@ -220,13 +230,13 @@ def tile_picked_joinbigpolarunder_none_po_kernel(
 
         def round_pair(u, c):
             j0, j1 = CHUNKS[c]
-            nc.scalar.copy(o_bf[c][:, :, 2 * u : 2 * u + 2], o[u][:, :, j0:j1].rearrange("p e j -> p j e"))
+            copy = nc.vector.tensor_copy if u == 1 and c == len(CHUNKS) - 1 else nc.scalar.copy
+            copy(o_bf[c][:, :, 2 * u : 2 * u + 2], o[u][:, :, j0:j1].rearrange("p e j -> p j e"))
 
         for t in range(PACK - 1):
             a = keep.tile([P, S], F32, name=f"a{t}")
             b = keep.tile([P, S], F32, name=f"b{t}")
-            for j0, j1 in HALVES:
-                differences(t, a, b, j0, j1)
+            differences(t, a, b, 0, S)
             nc.vector.tensor_tensor(o[t // 2][:, t % 2, :], a[:], b[:], ALU.max)
             nc.sync.dma_start(out_rows[:, t, :], o[t // 2][:, t % 2, :])
             if t == 1:

from contextlib import ExitStack

import concourse.mybir as mybir
from concourse.masks import make_identity

K, T, S, N, H, W = 512, 2048, 512, 512, 512, 256
FLOPS = 2 * K * H * S + 2 * 2 * H * N * S

F32 = mybir.dt.float32
BF16 = mybir.dt.bfloat16
I32 = mybir.dt.int32
U32 = mybir.dt.uint32
U16 = mybir.dt.uint16
U8 = mybir.dt.uint8
FP8X4 = mybir.dt.float8_e4m3fn_x4
FP4X4 = mybir.dt.float4_e2m1fn_x4
ALU = mybir.AluOpType
ACT = mybir.ActivationFunctionType

P = 128
PACK = 4
CHUNKS = ((0, 256), (256, 384), (384, 512))
HALVES = ((0, 256), (256, 512))


def tile_picked_joinbigpolarunder_none_po_kernel(
    tc, x_words, x_scales, w1_words, w1_scales, gn, gm, w2_words, w2_scales, w3_words, w3_scales,
    offs, n1, n2, n3, n4, n5, out_0, out_1, out_2,
):
    nc = tc.nc
    with ExitStack() as ctx:
        keep = ctx.enter_context(tc.tile_pool(name="keep", bufs=1))
        psum = ctx.enter_context(tc.psum_pool(name="psum", bufs=1))

        def load_list(name, src):
            tile = keep.tile([P, src.shape[1]], U16, name=name)
            nc.sync.dma_start(tile[:], src)
            return tile

        def zeroed_plane(name, tag, width):
            tile = keep.tile([P, width], U8, name=name, tag=tag, align_bytes=64)
            nc.gpsimd.memset(tile[:].bitcast(I32), 0)
            return tile

        def load_scales(queues, tile, src):
            for q, queue in enumerate(queues):
                queue.dma_start(tile[32 * q : 32 * q + 4, :].bitcast(I32), src[0, 4 * q : 4 * q + 4, :].bitcast(I32))

        def load_words(name, tag, src):
            tile = keep.tile([P, src.shape[2]], U8, name=name, tag=tag, align_bytes=64)
            nc.sync.dma_start(tile[:].bitcast(I32), src[0].bitcast(I32))
            return tile

        def load_gain(name, src):
            tile = keep.tile([P, PACK], F32, name=name)
            nc.gpsimd.dma_start(tile[:], src.rearrange("(p t) o -> p (t o)", t=PACK))
            return tile

        def deal_words(name, tag, raw, t0, t1):
            tile = keep.tile([P, (t1 - t0) * 2 * P], U8, name=name, tag=tag, align_bytes=64)
            nc.vector.tensor_copy(
                tile[:].rearrange("p (t m b) -> p t m b", m=P, b=2),
                raw[:].rearrange("p (m t b) -> p t m b", t=PACK, b=2)[:, t0:t1],
            )
            return tile

        def deal_scales(name, tag, raw, t0, t1):
            tile = keep.tile([P, (t1 - t0) * P], U8, name=name, tag=tag, align_bytes=64)
            nc.vector.tensor_copy(
                tile[:].rearrange("p (t m) -> p t m", m=P),
                raw[:].rearrange("p (m t) -> p t m", t=PACK)[:, t0:t1],
            )
            return tile

        def mx_pass(bank, words, scales, t, codes, code_scales, start, stop):
            nc.tensor.matmul_mx(
                out=bank,
                lhsT=words[:, 2 * P * t : 2 * P * (t + 1)].bitcast(FP4X4),
                lhsT_scale=scales[:, P * t : P * (t + 1)],
                rhs=codes.bitcast(FP8X4),
                rhs_scale=code_scales,
                start=start,
                stop=stop,
            )

        offs_t = load_list("offs_t", offs)
        w1_raw = load_words("w1_raw", "w1_raw", w1_words)
        x_raw = keep.tile([P, T], I32, name="x_raw", tag="x_raw", align_bytes=64)
        nc.sync.dma_start(x_raw[:], x_words[0].rearrange("p n r -> p (n r)").bitcast(I32))
        n2_t = load_list("n2_t", n2)
        n3_t = load_list("n3_t", n3)
        n1_t = load_list("n1_t", n1)
        n4_t = load_list("n4_t", n4)
        n5_t = load_list("n5_t", n5)
        xs_raw = zeroed_plane("xs_raw", "xs_raw", T)
        w1s_raw = zeroed_plane("w1s_raw", "w1s_raw", H)
        load_scales([nc.scalar, nc.scalar, nc.gpsimd, nc.gpsimd], xs_raw, x_scales)
        load_scales([nc.scalar] * 4, w1s_raw, w1_scales)
        ident = keep.tile([P, P], F32, name="ident", tag="ident", align_bytes=64)
        make_identity(nc, ident[:])
        gm_t = load_gain("gm_t", gm)
        gn_t = load_gain("gn_t", gn)

        w1 = deal_words("w1", "w1", w1_raw, 0, PACK)
        w3_raw = load_words("w3_raw", "w1_raw", w3_words)
        xw = keep.tile([P, S], U32, name="xw", align_bytes=64)
        nc.vector.tensor_copy(xw[:], x_raw[:].bitcast(U32).indirect(offs_t[:]))
        xs = keep.tile([P, S], U8, name="xs", tag="x_raw", align_bytes=64)
        nc.vector.tensor_copy(xs[:], xs_raw[:].indirect(offs_t[:]))
        w1s_first = deal_scales("w1s_first", "w1s_first", w1s_raw, 0, 1)
        w1s_rest = deal_scales("w1s_rest", "xs_raw", w1s_raw, 1, PACK)
        w3 = deal_words("w3", "w1s_raw", w3_raw, 0, PACK)
        w2_raw = load_words("w2_raw", "w1_raw", w2_words)

        y = []
        for t in range(PACK):
            bank = psum.tile([P, S], F32, name=f"ybank{t}", tag=f"bank{t}")
            scales = w1s_first[:] if t == 0 else w1s_rest[:, P * (t - 1) : P * t]
            mx_pass(bank[:], w1[:, 2 * P * t :], scales, 0, xw[:], xs[:], True, True)
            y_t = keep.tile([P, S], F32, name=f"y{t}")
            nc.scalar.copy(y_t[:], bank[:])
            y.append(y_t)

        w3s_raw = zeroed_plane("w3s_raw", "w1s_first", N)
        w2s_raw = zeroed_plane("w2s_raw", "w1", N)
        load_scales([nc.sync] * 4, w3s_raw, w3_scales)
        load_scales([nc.sync] * 4, w2s_raw, w2_scales)

        dt = []

        def pair_up(t):
            u = keep.tile([P, W], F32, name=f"half_pa{t}")
            nc.vector.tensor_scalar(u[:], y[t][:].indirect(n2_t[:]), -0.5, 0.0, ALU.mult, ALU.add)
            b = keep.tile([P, W], F32, name=f"pb{t}")
            nc.vector.tensor_copy(b[:], y[t][:].indirect(n3_t[:]))
            sq = keep.tile([P, S], F32, name=f"sq{t}", tag=f"sq{t}", align_bytes=64)
            nc.scalar.activation(sq[:, :W], u[:], ACT.Square, scale=2.0)
            nc.scalar.activation(sq[:, W:], b[:], ACT.Square)
            bank = psum.tile([P, 2, W], F32, name=f"rbank{t}", tag=f"bank{t}")
            for a in range(0, W, P):
                for e in range(2):
                    nc.tensor.matmul(bank[:, 0, a : a + P], sq[:, e * W + a : e * W + a + P], ident[:], start=e == 0, stop=e == 1, is_transpose=True)
            turned = keep.tile([P, W], F32, name=f"turned{t}", tag=f"turned{t}", align_bytes=64)
            nc.scalar.activation(turned[:], bank[:, 0, :], ACT.Sqrt, bias=0.25)
            for a in range(0, W, P):
                nc.tensor.transpose(bank[:, 1, a : a + P], turned[:, a : a + P], ident[:])
            r = keep.tile([P, W], F32, name=f"ra{t}", tag=f"ra{t}")
            nc.scalar.copy(r[:], bank[:, 1, :])
            return u, b, r

        def put_rb(t, u, b):
            d = keep.tile([P, S], F32, name=f"dt{t}", tag=("sq0", "sq1", "turned0", "turned1")[t], align_bytes=64)
            nc.vector.tensor_tensor(d[:].indirect(n3_t[:]), b[:], u[:], ALU.add)
            dt.append(d)

        def put_ra(t, r):
            nc.vector.tensor_copy(dt[t][:].indirect(n2_t[:]), r)
            nc.scalar.activation(z2_bf[:, :, t], dt[t][:], ACT.Copy, scale=gm_t[:, t : t + 1])

        pairs = [pair_up(t) for t in range(PACK)]
        for t in range(PACK):
            put_rb(t, pairs[t][0], pairs[t][1])
        z2_bf = keep.tile([P, S, PACK], BF16, name="z2_bf", tag="ident", align_bytes=64)
        for t in range(PACK):
            put_ra(t, pairs[t][2][:])
        w2_first = deal_words("w2_first", "sq1", w2_raw, 0, 1)
        w2s = deal_scales("w2s", "turned0", w2s_raw, 0, PACK)
        w3s = deal_scales("w3s", "turned1", w3s_raw, 0, PACK)
        z2_codes = keep.tile([P, S], U32, name="z2_codes", align_bytes=64)
        z2_scales = keep.tile([P, S], U8, name="z2_scales", align_bytes=64)
        nc.vector.quantize_mx(
            out=z2_codes[:].bitcast(FP8X4), scales=z2_scales[:], in_=z2_bf[:].rearrange("p j t -> p (j t)")
        )

        z_codes = keep.tile([P, S], U32, name="z_codes", align_bytes=64)
        z_scales = keep.tile([P, S], U8, name="z_scales", align_bytes=64)
        z_bf = [keep.tile([P, j1 - j0, PACK], BF16, name=f"z_bf{c}", tag=f"z_bf{c}", align_bytes=64) for c, (j0, j1) in enumerate(CHUNKS)]
        last = PACK - 1
        neg_h = [keep.tile([P, 2 * S if t < last else S], F32, name=f"neg_h{t}") for t in range(PACK)]
        h = [neg_h[1][:, S:], neg_h[2][:, S:], keep.tile([P, S], F32, name="h2")[:], keep.tile([P, S], F32, name="h3")[:]]
        fetched = keep.tile([P, PACK, S], F32, name="fetched", tag="ra3")
        for t in range(PACK - 1):
            g = fetched[:, t, :]
            for j0, j1 in HALVES:
                nc.vector.tensor_copy(g[:, j0:j1], y[t][:].indirect(n1_t[:, j0 // 16 : j1 // 16]))
            m = neg_h[0][:, S:] if t == 0 else keep.tile([P, S], F32, name=f"m{t}")[:]
            nc.vector.tensor_tensor(m, g, y[t][:], ALU.max)
            for c, (j0, j1) in enumerate(CHUNKS):
                nc.scalar.activation(z_bf[c][:, :, t], m[:, j0:j1], ACT.Copy, scale=gn_t[:, t : t + 1])
        g = fetched[:, last, :]
        m = keep.tile([P, S], F32, name="m3")
        banks = []
        for c, (j0, j1) in enumerate(CHUNKS):
            width = j1 - j0
            nc.vector.tensor_copy(g[:, j0:j1], y[last][:].indirect(n1_t[:, j0 // 16 : j1 // 16]))
            nc.vector.tensor_tensor(m[:, j0:j1], g[:, j0:j1], y[last][:, j0:j1], ALU.max)
            nc.scalar.activation(z_bf[c][:, :, last], m[:, j0:j1], ACT.Copy, scale=gn_t[:, last : last + 1])
            nc.vector.quantize_mx(
                out=z_codes[:, j0:j1].bitcast(FP8X4), scales=z_scales[:, j0:j1],
                in_=z_bf[c][:].rearrange("p j t -> p (j t)"),
            )
            bank = psum.tile([P, width], F32, name=f"h0bank{c}", tag=f"h0bank{c}")
            for a in range(j0, j1, P):
                cols = slice(a, a + P)
                mx_pass(bank[:, a - j0 : a - j0 + P], w3, w3s, 0, z2_codes[:, cols], z2_scales[:, cols], True, False)
                mx_pass(bank[:, a - j0 : a - j0 + P], w2_first, w2s, 0, z_codes[:, cols], z_scales[:, cols], False, True)
            banks.append(bank)
        for c, (j0, j1) in enumerate(CHUNKS):
            nc.scalar.activation(neg_h[0][:, j0:j1], banks[c][:], ACT.Copy, scale=-1.0)
            nc.scalar.copy(h[0][:, j0:j1], banks[c][:])

        w2_rest = deal_words("w2_rest", f"z_bf{len(CHUNKS) - 1}", w2_raw, 1, PACK)
        for t in range(1, PACK):
            bank = psum.tile([P, S], F32, name=f"hbank{t}", tag=f"bank{t}")
            mx_pass(bank[:], w3, w3s, t, z2_codes[:], z2_scales[:], True, False)
            mx_pass(bank[:], w2_rest, w2s[:, P:], t - 1, z_codes[:], z_scales[:], False, True)
            nc.scalar.activation(neg_h[t][:, :S], bank[:], ACT.Copy, scale=-1.0)
            nc.scalar.copy(h[t], bank[:])

        out_rows = out_0.rearrange("(p t) j -> p t j", t=PACK)
        out_words = out_1[0].rearrange("p j r -> p (j r)").bitcast(I32)
        o_codes = keep.tile([P, S], I32, name="o_codes", align_bytes=64)
        o_scales = keep.tile([P, S], U8, name="o_scales", align_bytes=64)
        o_bf = [keep.tile([P, j1 - j0, PACK], BF16, name=f"o_bf{c}", align_bytes=64) for c, (j0, j1) in enumerate(CHUNKS)]
        o = [keep.tile([P, 2, S], F32, name=f"o{u}") for u in range(2)]

        def differences(t, a, b, j0, j1):
            nc.vector.tensor_tensor(a[:, j0:j1], neg_h[t][:].indirect(n4_t[:, j0 // 16 : j1 // 16]), h[t][:, j0:j1], ALU.add)
            nc.vector.tensor_tensor(b[:, j0:j1], neg_h[t][:].indirect(n5_t[:, j0 // 16 : j1 // 16]), h[t][:, j0:j1], ALU.add)

        def round_pair(u, c):
            j0, j1 = CHUNKS[c]
            copy = nc.vector.tensor_copy if u == 1 and c == len(CHUNKS) - 1 else nc.scalar.copy
            copy(o_bf[c][:, :, 2 * u : 2 * u + 2], o[u][:, :, j0:j1].rearrange("p e j -> p j e"))

        for t in range(PACK - 1):
            a = keep.tile([P, S], F32, name=f"a{t}")
            b = keep.tile([P, S], F32, name=f"b{t}")
            differences(t, a, b, 0, S)
            nc.vector.tensor_tensor(o[t // 2][:, t % 2, :], a[:], b[:], ALU.max)
            nc.sync.dma_start(out_rows[:, t, :], o[t // 2][:, t % 2, :])
            if t == 1:
                for c in range(len(CHUNKS)):
                    round_pair(0, c)
        a = keep.tile([P, S], F32, name="a3")
        b = keep.tile([P, S], F32, name="b3")
        for c, (j0, j1) in enumerate(CHUNKS):
            differences(last, a, b, j0, j1)
            nc.vector.tensor_tensor(o[1][:, 1, j0:j1], a[:, j0:j1], b[:, j0:j1], ALU.max)
            nc.sync.dma_start(out_rows[:, last, j0:j1], o[1][:, 1, j0:j1])
            round_pair(1, c)
            nc.vector.quantize_mx(
                out=o_codes[:, j0:j1].bitcast(FP8X4), scales=o_scales[:, j0:j1],
                in_=o_bf[c][:].rearrange("p j t -> p (j t)"),
            )
            nc.sync.dma_start(out_words[:, j0:j1], o_codes[:, j0:j1])
        for q in range(4):
            queue = nc.scalar if q % 2 else nc.sync
            queue.dma_start(out_2[0, 4 * q : 4 * q + 4, :].bitcast(I32), o_scales[32 * q : 32 * q + 4, :].bitcast(I32))
